import numpy as np
import ml_dtypes


def mxq(x, axis, fmt="e4m3"):
    dtype, down = {"e4m3": (ml_dtypes.float8_e4m3fn, 7), "e5m2": (ml_dtypes.float8_e5m2, 14)}[fmt]
    v = np.moveaxis(np.asarray(x, np.float32).astype(ml_dtypes.bfloat16).astype(np.float64), axis, -1)
    blocks = v.reshape(v.shape[:-1] + (-1, 32))
    amax = np.abs(blocks).max(-1, keepdims=True)
    byte = np.maximum(np.where(amax > 0, np.frexp(amax)[1] - 1 + 127, 0) - down, 1)
    scale = np.exp2(byte - 127.0)
    codes = (blocks / scale).astype(np.float32).astype(dtype).astype(np.float64)
    return np.moveaxis((codes * scale).reshape(v.shape), -1, axis)


WIDE = False


def mx_kscale(k, group=512):
    if not WIDE:
        return np.ones(k)
    levels = np.array([18, -18])
    if group != 512:
        return np.exp2(np.random.permutation(np.resize(levels, k // group))).repeat(group)
    if k % 512:
        return np.exp2(np.random.permutation(np.resize(levels, k // 32))).repeat(32)
    a = np.empty((k // 512, 16))
    for p in range(k // 512):
        a[p, :8] = np.random.permutation(np.resize(levels, 8))
        for g in range(8):
            far = levels[np.abs(levels - a[p, g]) >= 10]
            a[p, g + 8] = far[np.random.randint(len(far))]
    return np.exp2(a.ravel()).repeat(32)


def f64(x):
    return np.asarray(x).astype(np.float64)


G, D, M, N = 4, 128, 256, 512


def setup_inputs():
    n = np.random.standard_normal
    s_d = mx_kscale(D, 0)
    return {
        "x": (n((G, D, M)) / s_d[:, None] / np.sqrt(D)).astype(np.float32),
        "c": (n((G, D, N)) * s_d[:, None] / np.sqrt(D)).astype(np.float32),
        "xn": (np.random.uniform(0.9, 1.3, (G, M, 1))).astype(np.float32),
        "cn": (np.random.uniform(0.9, 1.3, (G, 1, N))).astype(np.float32),
    }


def reference(x, c, xn, cn):
    xq = mxq(f64(x), 1, "e4m3")
    cq = mxq(f64(c), 1, "e4m3")
    z = xq.transpose(0, 2, 1) @ cq
    d2 = f64(xn) + f64(cn) - 2.0 * z
    t = 1.0 / (1.0 + d2)
    rs = np.sum(t, axis=-1, keepdims=True)
    y = t / rs
    return y

@@ -1,0 +1,151 @@
+from contextlib import ExitStack
+
+import concourse.mybir as mybir
+
+G, D, M, N = 4, 128, 256, 512
+FLOPS = 2 * G * D * M * N
+
+F32 = mybir.dt.float32
+BF16 = mybir.dt.bfloat16
+U32 = mybir.dt.uint32
+U8 = mybir.dt.uint8
+FP8X4 = mybir.dt.float8_e4m3fn_x4
+ALU = mybir.AluOpType
+ACT = mybir.ActivationFunctionType
+
+P = 128
+PACK = 4
+ROWS = D // PACK
+HALVES = M // P
+C_SPLIT = 320
+SCALE_ON_VECTOR = (7,)
+
+
+def tile_rows_kern_student_kernel(tc, x, c, xn, cn, out):
+    nc = tc.nc
+    tiles = [(g, h) for g in range(G) for h in range(HALVES)]
+    T = len(tiles)
+
+    with ExitStack() as ctx:
+        pool = ctx.enter_context(tc.tile_pool(name="sb", bufs=1))
+        psum = ctx.enter_context(tc.psum_pool(name="ps", bufs=1))
+        ctx.enter_context(tc.manual_schedule())
+
+        c_raw = pool.tile([P, PACK, N], F32, name="c_raw")
+        x_raw = pool.tile([P, PACK, M], F32, name="x_raw")
+        xn_sb = pool.tile([P, G, HALVES], F32, name="xn_sb")
+        cn_sb = [pool.tile([P, N], F32, name="cn%d" % g) for g in range(G)]
+
+        nc.scalar.dma_start(out=xn_sb[:], in_=xn.rearrange("g (p h) o -> p g (h o)", h=HALVES))
+        nc.sync.dma_start(out=c_raw[:], in_=c.rearrange("g (p j) n -> (g p) j n", j=PACK))
+        nc.sync.dma_start(out=x_raw[:], in_=x.rearrange("g (p j) m -> (g p) j m", j=PACK))
+        for g in range(G):
+            nc.sync.dma_start(out=cn_sb[g][:], in_=cn[g, 0, :].partition_broadcast(P))
+
+        c_bf = pool.tile([P, N, PACK], BF16, name="c_bf", align_bytes=64)
+        c_codes = pool.tile([P, N], U32, name="c_codes", align_bytes=64)
+        c_scales = pool.tile([P, N], U8, name="c_scales", align_bytes=64)
+        x_bf = [pool.tile([P, P, PACK], BF16, name="x_bf%d" % h, align_bytes=64) for h in range(HALVES)]
+        x_codes = [pool.tile([P, P], U32, name="x_codes%d" % h, align_bytes=64) for h in range(HALVES)]
+        x_scales = [pool.tile([P, P], U8, name="x_scales%d" % h, align_bytes=64) for h in range(HALVES)]
+
+        def c_cols(lo, hi):
+            return c_bf[:, lo:hi, :], c_raw[:, :, lo:hi].rearrange("p j n -> p n j")
+
+        def x_half(h):
+            return x_bf[h][:], x_raw[:].rearrange("p j (m h) -> p h m j", h=HALVES)[:, h, :, :]
+
+        def quantize_c(lo, hi):
+            nc.vector.quantize_mx(
+                out=c_codes[:, lo:hi].bitcast(FP8X4),
+                scales=c_scales[:, lo:hi],
+                in_=c_bf[:, lo:hi, :].rearrange("p n j -> p (n j)"),
+            )
+
+        def quantize_x(h):
+            nc.vector.quantize_mx(
+                out=x_codes[h][:].bitcast(FP8X4),
+                scales=x_scales[h][:],
+                in_=x_bf[h][:].rearrange("p m j -> p (m j)"),
+            )
+
+        nc.vector.tensor_copy(*c_cols(0, N // 2))
+        nc.scalar.copy(*c_cols(C_SPLIT, N))
+        nc.vector.tensor_copy(*c_cols(N // 2, C_SPLIT))
+        quantize_c(0, N // 2)
+        nc.vector.tensor_copy(*x_half(0))
+        quantize_c(N // 2, N)
+        quantize_x(0)
+        nc.vector.tensor_copy(*x_half(1))
+        bias = pool.tile([P, T], F32, name="bias")
+        neg_bias = pool.tile([P, T], F32, name="neg_bias")
+        xn_flat = xn_sb[:].rearrange("p g h -> p (g h)")
+        nc.vector.tensor_scalar(out=bias[:], in0=xn_flat, scalar1=1.0, scalar2=None, op0=ALU.add)
+        nc.vector.tensor_scalar(out=neg_bias[:], in0=xn_flat, scalar1=1.0, scalar2=-1.0, op0=ALU.add, op1=ALU.mult)
+
+        quantize_x(1)
+
+        z = {}
+        for g in range(G):
+            for h in range(HALVES):
+                rows = slice(ROWS * g, ROWS * (g + 1))
+                z[g, h] = psum.tile([P, N], F32, name="z%d_%d" % (g, h))
+                nc.tensor.matmul_mx(
+                    out=z[g, h][:],
+                    lhsT=x_codes[h][rows, :].bitcast(FP8X4),
+                    lhsT_scale=x_scales[h][rows, :],
+                    rhs=c_codes[rows, :].bitcast(FP8X4),
+                    rhs_scale=c_scales[rows, :],
+                    start=True,
+                    stop=True,
+                )
+
+        part = [pool.tile([P, N], F32, name="part%d" % i) for i in range(T)]
+        root = [pool.tile([P, N], F32, name="root%d" % i) for i in range(T)]
+        mag = [pool.tile([P, N], F32, name="mag%d" % i) for i in range(T)]
+        half_sign = [pool.tile([P, N], BF16, name="half_sign%d" % i) for i in range(T)]
+        t = [pool.tile([P, N], F32, name="t%d" % i) for i in range(T)]
+        y = [pool.tile([P, N], F32, name="y%d" % i) for i in range(T)]
+        row_sum = [pool.tile([P, 1], F32, name="row_sum%d" % i) for i in range(T)]
+        inv_sum = [pool.tile([P, 1], F32, name="inv_sum%d" % i) for i in range(T)]
+
+        def distance(i):
+            g, h = tiles[i]
+            nc.vector.scalar_tensor_tensor(
+                out=part[i][:], in0=z[g, h][:], scalar=-2.0, in1=cn_sb[g][:], op0=ALU.mult, op1=ALU.add
+            )
+
+        def inverse_root(i):
+            nc.scalar.activation(out=root[i][:], in_=part[i][:], func=ACT.Abs_reciprocal_sqrt, bias=bias[:, i : i + 1])
+
+        def square(i):
+            nc.scalar.activation(out=mag[i][:], in_=root[i][:], func=ACT.Square)
+
+        def sign(i):
+            nc.vector.tensor_scalar(
+                out=half_sign[i][:], in0=part[i][:], scalar1=neg_bias[:, i : i + 1], scalar2=0.5,
+                op0=ALU.is_ge, op1=ALU.subtract,
+            )
+
+        def signed_sum(i):
+            nc.vector.scalar_tensor_tensor(
+                out=t[i][:], in0=mag[i][:], scalar=2.0, in1=half_sign[i][:], op0=ALU.mult, op1=ALU.mult,
+                accum_out=row_sum[i][:],
+            )
+
+        def invert_sum(i):
+            nc.vector.reciprocal(out=inv_sum[i][:], in_=row_sum[i][:])
+
+        def normalise(i):
+            g, h = tiles[i]
+            if i in SCALE_ON_VECTOR:
+                nc.vector.tensor_scalar(out=y[i][:], in0=t[i][:], scalar1=inv_sum[i][:], scalar2=None, op0=ALU.mult)
+            else:
+                nc.scalar.activation(out=y[i][:], in_=t[i][:], func=ACT.Copy, scale=inv_sum[i][:])
+            nc.sync.dma_start(out=out[g].rearrange("(p h) n -> p h n", h=HALVES)[:, h, :], in_=y[i][:])
+
+        stages = [(distance, -1), (signed_sum, 1), (sign, -1), (invert_sum, 1), (inverse_root, 0), (normalise, 2), (square, 0)]
+        for step in range(-1, T + 2):
+            for stage, lag in stages:
+                if 0 <= step - lag < T:
+                    stage(step - lag)

@@ -17,8 +17,11 @@ P = 128
 PACK = 4
 ROWS = D // PACK
 HALVES = M // P
+BLOCK = 32
+XN_STEP = BLOCK // (G * HALVES)
+FAN = 8
 C_SPLIT = 320
-SCALE_ON_VECTOR = (7,)
+SCALE_ON_VECTOR = (5, 6, 7)
 
 
 def tile_rows_kern_student_kernel(tc, x, c, xn, cn, out):
@@ -33,14 +36,22 @@ def tile_rows_kern_student_kernel(tc, x, c, xn, cn, out):
 
         c_raw = pool.tile([P, PACK, N], F32, name="c_raw")
         x_raw = pool.tile([P, PACK, M], F32, name="x_raw")
-        xn_sb = pool.tile([P, G, HALVES], F32, name="xn_sb")
+        xn_rows = pool.tile([P, BLOCK], F32, name="xn_rows", align_bytes=64)
+        xn_cols = pool.tile([P, BLOCK], F32, name="xn_cols", align_bytes=64)
+        cn_seed = pool.tile([P, G * N], F32, name="cn_seed")
         cn_sb = [pool.tile([P, N], F32, name="cn%d" % g) for g in range(G)]
 
-        nc.scalar.dma_start(out=xn_sb[:], in_=xn.rearrange("g (p h) o -> p g (h o)", h=HALVES))
+        nc.scalar.dma_start(
+            out=cn_seed[0:P:FAN, :], in_=cn.rearrange("g o n -> o (g n)")[0, :].partition_broadcast(P // FAN)
+        )
+        nc.vector.memset(xn_rows[:], 0.0)
+        nc.scalar.dma_start(
+            out=xn_rows[0:P:XN_STEP, :], in_=xn.rearrange("g (h q a) o -> q (g h) (a o)", h=HALVES, a=BLOCK)
+        )
         nc.sync.dma_start(out=c_raw[:], in_=c.rearrange("g (p j) n -> (g p) j n", j=PACK))
         nc.sync.dma_start(out=x_raw[:], in_=x.rearrange("g (p j) m -> (g p) j m", j=PACK))
         for g in range(G):
-            nc.sync.dma_start(out=cn_sb[g][:], in_=cn[g, 0, :].partition_broadcast(P))
+            nc.sync.dma_start(out=cn_sb[g][:], in_=cn_seed[0:P:FAN, g * N : (g + 1) * N].unsqueeze(1).to_broadcast([P // FAN, FAN, N]))
 
         c_bf = pool.tile([P, N, PACK], BF16, name="c_bf", align_bytes=64)
         c_codes = pool.tile([P, N], U32, name="c_codes", align_bytes=64)
@@ -53,7 +64,7 @@ def tile_rows_kern_student_kernel(tc, x, c, xn, cn, out):
             return c_bf[:, lo:hi, :], c_raw[:, :, lo:hi].rearrange("p j n -> p n j")
 
         def x_half(h):
-            return x_bf[h][:], x_raw[:].rearrange("p j (m h) -> p h m j", h=HALVES)[:, h, :, :]
+            return x_bf[h][:], x_raw[:, :, h * P : (h + 1) * P].rearrange("p j m -> p m j")
 
         def quantize_c(lo, hi):
             nc.vector.quantize_mx(
@@ -78,12 +89,9 @@ def tile_rows_kern_student_kernel(tc, x, c, xn, cn, out):
         quantize_x(0)
         nc.vector.tensor_copy(*x_half(1))
         bias = pool.tile([P, T], F32, name="bias")
-        neg_bias = pool.tile([P, T], F32, name="neg_bias")
-        xn_flat = xn_sb[:].rearrange("p g h -> p (g h)")
-        nc.vector.tensor_scalar(out=bias[:], in0=xn_flat, scalar1=1.0, scalar2=None, op0=ALU.add)
-        nc.vector.tensor_scalar(out=neg_bias[:], in0=xn_flat, scalar1=1.0, scalar2=-1.0, op0=ALU.add, op1=ALU.mult)
-
+        nc.vector.transpose(out=xn_cols[:], in_=xn_rows[:])
         quantize_x(1)
+        nc.vector.tensor_scalar(out=bias[:], in0=xn_cols[:, 0:BLOCK:XN_STEP], scalar1=1.0, scalar2=None, op0=ALU.add)
 
         z = {}
         for g in range(G):
@@ -103,7 +111,7 @@ def tile_rows_kern_student_kernel(tc, x, c, xn, cn, out):
         part = [pool.tile([P, N], F32, name="part%d" % i) for i in range(T)]
         root = [pool.tile([P, N], F32, name="root%d" % i) for i in range(T)]
         mag = [pool.tile([P, N], F32, name="mag%d" % i) for i in range(T)]
-        half_sign = [pool.tile([P, N], BF16, name="half_sign%d" % i) for i in range(T)]
+        positive = [pool.tile([P, N], BF16, name="positive%d" % i) for i in range(T)]
         t = [pool.tile([P, N], F32, name="t%d" % i) for i in range(T)]
         y = [pool.tile([P, N], F32, name="y%d" % i) for i in range(T)]
         row_sum = [pool.tile([P, 1], F32, name="row_sum%d" % i) for i in range(T)]
@@ -123,13 +131,13 @@ def tile_rows_kern_student_kernel(tc, x, c, xn, cn, out):
 
         def sign(i):
             nc.vector.tensor_scalar(
-                out=half_sign[i][:], in0=part[i][:], scalar1=neg_bias[:, i : i + 1], scalar2=0.5,
-                op0=ALU.is_ge, op1=ALU.subtract,
+                out=positive[i][:], in0=part[i][:], scalar1=bias[:, i : i + 1], scalar2=0.0,
+                op0=ALU.add, op1=ALU.is_ge,
             )
 
         def signed_sum(i):
             nc.vector.scalar_tensor_tensor(
-                out=t[i][:], in0=mag[i][:], scalar=2.0, in1=half_sign[i][:], op0=ALU.mult, op1=ALU.mult,
+                out=t[i][:], in0=positive[i][:], scalar=0.5, in1=mag[i][:], op0=ALU.subtract, op1=ALU.mult,
                 accum_out=row_sum[i][:],
             )
 
@@ -142,10 +150,10 @@ def tile_rows_kern_student_kernel(tc, x, c, xn, cn, out):
                 nc.vector.tensor_scalar(out=y[i][:], in0=t[i][:], scalar1=inv_sum[i][:], scalar2=None, op0=ALU.mult)
             else:
                 nc.scalar.activation(out=y[i][:], in_=t[i][:], func=ACT.Copy, scale=inv_sum[i][:])
-            nc.sync.dma_start(out=out[g].rearrange("(p h) n -> p h n", h=HALVES)[:, h, :], in_=y[i][:])
+            nc.sync.dma_start(out=out[g, h * P : (h + 1) * P, :], in_=y[i][:])
 
-        stages = [(distance, -1), (signed_sum, 1), (sign, -1), (invert_sum, 1), (inverse_root, 0), (normalise, 2), (square, 0)]
-        for step in range(-1, T + 2):
+        stages = [(distance, 0), (signed_sum, 3), (sign, 1), (inverse_root, 0), (square, 1), (normalise, 4), (invert_sum, 3)]
+        for step in range(T + 4):
             for stage, lag in stages:
                 if 0 <= step - lag < T:
                     stage(step - lag)

@@ -21,7 +21,8 @@ BLOCK = 32
 XN_STEP = BLOCK // (G * HALVES)
 FAN = 8
 C_SPLIT = 320
-SCALE_ON_VECTOR = (5, 6, 7)
+SIGNS_ON_GPSIMD = 4
+TINY = 2.0**-100
 
 
 def tile_rows_kern_student_kernel(tc, x, c, xn, cn, out):
@@ -63,8 +64,11 @@ def tile_rows_kern_student_kernel(tc, x, c, xn, cn, out):
         def c_cols(lo, hi):
             return c_bf[:, lo:hi, :], c_raw[:, :, lo:hi].rearrange("p j n -> p n j")
 
-        def x_half(h):
-            return x_bf[h][:], x_raw[:, :, h * P : (h + 1) * P].rearrange("p j m -> p m j")
+        def cast_x(h):
+            nc.vector.tensor_scalar(
+                out=x_bf[h][:], in0=x_raw[:, :, h * P : (h + 1) * P].rearrange("p j m -> p m j"),
+                scalar1=-2.0, scalar2=None, op0=ALU.mult,
+            )
 
         def quantize_c(lo, hi):
             nc.vector.quantize_mx(
@@ -84,10 +88,10 @@ def tile_rows_kern_student_kernel(tc, x, c, xn, cn, out):
         nc.scalar.copy(*c_cols(C_SPLIT, N))
         nc.vector.tensor_copy(*c_cols(N // 2, C_SPLIT))
         quantize_c(0, N // 2)
-        nc.vector.tensor_copy(*x_half(0))
+        cast_x(0)
         quantize_c(N // 2, N)
         quantize_x(0)
-        nc.vector.tensor_copy(*x_half(1))
+        cast_x(1)
         bias = pool.tile([P, T], F32, name="bias")
         nc.vector.transpose(out=xn_cols[:], in_=xn_rows[:])
         quantize_x(1)
@@ -120,40 +124,63 @@ def tile_rows_kern_student_kernel(tc, x, c, xn, cn, out):
         def distance(i):
             g, h = tiles[i]
             nc.vector.scalar_tensor_tensor(
-                out=part[i][:], in0=z[g, h][:], scalar=-2.0, in1=cn_sb[g][:], op0=ALU.mult, op1=ALU.add
+                out=part[i][:], in0=z[g, h][:], scalar=bias[:, i : i + 1], in1=cn_sb[g][:], op0=ALU.add, op1=ALU.add
             )
 
         def inverse_root(i):
-            nc.scalar.activation(out=root[i][:], in_=part[i][:], func=ACT.Abs_reciprocal_sqrt, bias=bias[:, i : i + 1])
+            nc.scalar.activation(out=root[i][:], in_=part[i][:], func=ACT.Abs_reciprocal_sqrt)
 
         def square(i):
             nc.scalar.activation(out=mag[i][:], in_=root[i][:], func=ACT.Square)
 
-        def sign(i):
-            nc.vector.tensor_scalar(
-                out=positive[i][:], in0=part[i][:], scalar1=bias[:, i : i + 1], scalar2=0.0,
-                op0=ALU.add, op1=ALU.is_ge,
+        def sign(i, engine):
+            engine.tensor_scalar(
+                out=positive[i][:], in0=part[i][:], scalar1=TINY, scalar2=-TINY, op0=ALU.min, op1=ALU.max
             )
+
+        def sign_on_gpsimd(i):
+            if i < SIGNS_ON_GPSIMD:
+                sign(i, nc.gpsimd)
+
+        def sign_on_vector(i):
+            if i >= SIGNS_ON_GPSIMD:
+                sign(i, nc.vector)
 
         def signed_sum(i):
             nc.vector.scalar_tensor_tensor(
-                out=t[i][:], in0=positive[i][:], scalar=0.5, in1=mag[i][:], op0=ALU.subtract, op1=ALU.mult,
+                out=t[i][:], in0=positive[i][:], scalar=1.0 / TINY, in1=mag[i][:], op0=ALU.mult, op1=ALU.mult,
                 accum_out=row_sum[i][:],
             )
 
         def invert_sum(i):
             nc.vector.reciprocal(out=inv_sum[i][:], in_=row_sum[i][:])
 
-        def normalise(i):
+        def store(i):
             g, h = tiles[i]
-            if i in SCALE_ON_VECTOR:
-                nc.vector.tensor_scalar(out=y[i][:], in0=t[i][:], scalar1=inv_sum[i][:], scalar2=None, op0=ALU.mult)
-            else:
-                nc.scalar.activation(out=y[i][:], in_=t[i][:], func=ACT.Copy, scale=inv_sum[i][:])
             nc.sync.dma_start(out=out[g, h * P : (h + 1) * P, :], in_=y[i][:])
 
-        stages = [(distance, 0), (signed_sum, 3), (sign, 1), (inverse_root, 0), (square, 1), (normalise, 4), (invert_sum, 3)]
-        for step in range(T + 4):
+        def normalise_on_vector(i):
+            if i % 2 == 1:
+                nc.vector.tensor_scalar(out=y[i][:], in0=t[i][:], scalar1=inv_sum[i][:], scalar2=None, op0=ALU.mult)
+                store(i)
+
+        def normalise_on_scalar(i):
+            if i % 2 == 0:
+                nc.scalar.activation(out=y[i][:], in_=t[i][:], func=ACT.Copy, scale=inv_sum[i][:])
+                store(i)
+
+        stages = [
+            (distance, 0),
+            (sign_on_gpsimd, 0),
+            (signed_sum, 6),
+            (sign_on_vector, 2),
+            (normalise_on_vector, 7),
+            (invert_sum, 6),
+            (inverse_root, 2),
+            (square, 3),
+            (normalise_on_scalar, 6),
+        ]
+        for step in range(T + 7):
             for stage, lag in stages:
                 if 0 <= step - lag < T:
                     stage(step - lag)

@@ -20,6 +20,7 @@ HALVES = M // P
 BLOCK = 32
 XN_STEP = BLOCK // (G * HALVES)
 FAN = 8
+RUN = 4
 C_SPLIT = 320
 SIGNS_ON_GPSIMD = 4
 TINY = 2.0**-100
@@ -62,11 +63,15 @@ def tile_rows_kern_student_kernel(tc, x, c, xn, cn, out):
         x_scales = [pool.tile([P, P], U8, name="x_scales%d" % h, align_bytes=64) for h in range(HALVES)]
 
         def c_cols(lo, hi):
-            return c_bf[:, lo:hi, :], c_raw[:, :, lo:hi].rearrange("p j n -> p n j")
+            return (
+                c_bf[:, lo:hi, :].rearrange("p (b i) j -> p b j i", i=RUN),
+                c_raw[:, :, lo:hi].rearrange("p j (b i) -> p b j i", i=RUN),
+            )
 
         def cast_x(h):
             nc.vector.tensor_scalar(
-                out=x_bf[h][:], in0=x_raw[:, :, h * P : (h + 1) * P].rearrange("p j m -> p m j"),
+                out=x_bf[h][:].rearrange("p (b i) j -> p b j i", i=RUN),
+                in0=x_raw[:, :, h * P : (h + 1) * P].rearrange("p j (b i) -> p b j i", i=RUN),
                 scalar1=-2.0, scalar2=None, op0=ALU.mult,
             )
 

@@ -68,12 +68,19 @@ def tile_rows_kern_student_kernel(tc, x, c, xn, cn, out):
                 c_raw[:, :, lo:hi].rearrange("p j (b i) -> p b j i", i=RUN),
             )
 
-        def cast_x(h):
-            nc.vector.tensor_scalar(
-                out=x_bf[h][:].rearrange("p (b i) j -> p b j i", i=RUN),
-                in0=x_raw[:, :, h * P : (h + 1) * P].rearrange("p j (b i) -> p b j i", i=RUN),
-                scalar1=-2.0, scalar2=None, op0=ALU.mult,
+        def x_cols(h, lo, hi):
+            return (
+                x_bf[h][:, lo:hi, :].rearrange("p (b i) j -> p b j i", i=RUN),
+                x_raw[:, :, h * P + lo : h * P + hi].rearrange("p j (b i) -> p b j i", i=RUN),
             )
+
+        def cast_x_on_vector(h, lo, hi):
+            dst, src = x_cols(h, lo, hi)
+            nc.vector.tensor_scalar(out=dst, in0=src, scalar1=-2.0, scalar2=None, op0=ALU.mult)
+
+        def cast_x_on_scalar(h, lo, hi):
+            dst, src = x_cols(h, lo, hi)
+            nc.scalar.activation(out=dst, in_=src, func=ACT.Copy, scale=-2.0)
 
         def quantize_c(lo, hi):
             nc.vector.quantize_mx(
@@ -93,14 +100,15 @@ def tile_rows_kern_student_kernel(tc, x, c, xn, cn, out):
         nc.scalar.copy(*c_cols(C_SPLIT, N))
         nc.vector.tensor_copy(*c_cols(N // 2, C_SPLIT))
         quantize_c(0, N // 2)
-        cast_x(0)
+        cast_x_on_vector(0, 0, P // 2)
+        cast_x_on_scalar(0, P // 2, P)
+        cast_x_on_scalar(1, 0, P)
         quantize_c(N // 2, N)
         quantize_x(0)
-        cast_x(1)
         bias = pool.tile([P, T], F32, name="bias")
         nc.vector.transpose(out=xn_cols[:], in_=xn_rows[:])
-        quantize_x(1)
         nc.vector.tensor_scalar(out=bias[:], in0=xn_cols[:, 0:BLOCK:XN_STEP], scalar1=1.0, scalar2=None, op0=ALU.add)
+        quantize_x(1)
 
         z = {}
         for g in range(G):

from contextlib import ExitStack

import concourse.mybir as mybir

G, D, M, N = 4, 128, 256, 512
FLOPS = 2 * G * D * M * N

F32 = mybir.dt.float32
BF16 = mybir.dt.bfloat16
U32 = mybir.dt.uint32
U8 = mybir.dt.uint8
FP8X4 = mybir.dt.float8_e4m3fn_x4
ALU = mybir.AluOpType
ACT = mybir.ActivationFunctionType

P = 128
PACK = 4
ROWS = D // PACK
HALVES = M // P
BLOCK = 32
XN_STEP = BLOCK // (G * HALVES)
FAN = 8
RUN = 4
C_SPLIT = 320
SIGNS_ON_GPSIMD = 4
TINY = 2.0**-100


def tile_rows_kern_student_kernel(tc, x, c, xn, cn, out):
    nc = tc.nc
    tiles = [(g, h) for g in range(G) for h in range(HALVES)]
    T = len(tiles)

    with ExitStack() as ctx:
        pool = ctx.enter_context(tc.tile_pool(name="sb", bufs=1))
        psum = ctx.enter_context(tc.psum_pool(name="ps", bufs=1))
        ctx.enter_context(tc.manual_schedule())

        c_raw = pool.tile([P, PACK, N], F32, name="c_raw")
        x_raw = pool.tile([P, PACK, M], F32, name="x_raw")
        xn_rows = pool.tile([P, BLOCK], F32, name="xn_rows", align_bytes=64)
        xn_cols = pool.tile([P, BLOCK], F32, name="xn_cols", align_bytes=64)
        cn_seed = pool.tile([P, G * N], F32, name="cn_seed")
        cn_sb = [pool.tile([P, N], F32, name="cn%d" % g) for g in range(G)]

        nc.scalar.dma_start(
            out=cn_seed[0:P:FAN, :], in_=cn.rearrange("g o n -> o (g n)")[0, :].partition_broadcast(P // FAN)
        )
        nc.vector.memset(xn_rows[:], 0.0)
        nc.scalar.dma_start(
            out=xn_rows[0:P:XN_STEP, :], in_=xn.rearrange("g (h q a) o -> q (g h) (a o)", h=HALVES, a=BLOCK)
        )
        nc.sync.dma_start(out=c_raw[:], in_=c.rearrange("g (p j) n -> (g p) j n", j=PACK))
        nc.sync.dma_start(out=x_raw[:], in_=x.rearrange("g (p j) m -> (g p) j m", j=PACK))
        for g in range(G):
            nc.sync.dma_start(out=cn_sb[g][:], in_=cn_seed[0:P:FAN, g * N : (g + 1) * N].unsqueeze(1).to_broadcast([P // FAN, FAN, N]))

        c_bf = pool.tile([P, N, PACK], BF16, name="c_bf", align_bytes=64)
        c_codes = pool.tile([P, N], U32, name="c_codes", align_bytes=64)
        c_scales = pool.tile([P, N], U8, name="c_scales", align_bytes=64)
        x_bf = [pool.tile([P, P, PACK], BF16, name="x_bf%d" % h, align_bytes=64) for h in range(HALVES)]
        x_codes = [pool.tile([P, P], U32, name="x_codes%d" % h, align_bytes=64) for h in range(HALVES)]
        x_scales = [pool.tile([P, P], U8, name="x_scales%d" % h, align_bytes=64) for h in range(HALVES)]

        def c_cols(lo, hi):
            return (
                c_bf[:, lo:hi, :].rearrange("p (b i) j -> p b j i", i=RUN),
                c_raw[:, :, lo:hi].rearrange("p j (b i) -> p b j i", i=RUN),
            )

        def x_cols(h, lo, hi):
            return (
                x_bf[h][:, lo:hi, :].rearrange("p (b i) j -> p b j i", i=RUN),
                x_raw[:, :, h * P + lo : h * P + hi].rearrange("p j (b i) -> p b j i", i=RUN),
            )

        def cast_x_on_vector(h, lo, hi):
            dst, src = x_cols(h, lo, hi)
            nc.vector.tensor_scalar(out=dst, in0=src, scalar1=-2.0, scalar2=None, op0=ALU.mult)

        def cast_x_on_scalar(h, lo, hi):
            dst, src = x_cols(h, lo, hi)
            nc.scalar.activation(out=dst, in_=src, func=ACT.Copy, scale=-2.0)

        def quantize_c(lo, hi):
            nc.vector.quantize_mx(
                out=c_codes[:, lo:hi].bitcast(FP8X4),
                scales=c_scales[:, lo:hi],
                in_=c_bf[:, lo:hi, :].rearrange("p n j -> p (n j)"),
            )

        def quantize_x(h):
            nc.vector.quantize_mx(
                out=x_codes[h][:].bitcast(FP8X4),
                scales=x_scales[h][:],
                in_=x_bf[h][:].rearrange("p m j -> p (m j)"),
            )

        nc.vector.tensor_copy(*c_cols(0, N // 2))
        nc.scalar.copy(*c_cols(C_SPLIT, N))
        nc.vector.tensor_copy(*c_cols(N // 2, C_SPLIT))
        quantize_c(0, N // 2)
        cast_x_on_vector(0, 0, P // 2)
        cast_x_on_scalar(0, P // 2, P)
        cast_x_on_scalar(1, 0, P)
        quantize_c(N // 2, N)
        quantize_x(0)
        bias = pool.tile([P, T], F32, name="bias")
        nc.vector.transpose(out=xn_cols[:], in_=xn_rows[:])
        nc.vector.tensor_scalar(out=bias[:], in0=xn_cols[:, 0:BLOCK:XN_STEP], scalar1=1.0, scalar2=None, op0=ALU.add)
        quantize_x(1)

        z = {}
        for g in range(G):
            for h in range(HALVES):
                rows = slice(ROWS * g, ROWS * (g + 1))
                z[g, h] = psum.tile([P, N], F32, name="z%d_%d" % (g, h))
                nc.tensor.matmul_mx(
                    out=z[g, h][:],
                    lhsT=x_codes[h][rows, :].bitcast(FP8X4),
                    lhsT_scale=x_scales[h][rows, :],
                    rhs=c_codes[rows, :].bitcast(FP8X4),
                    rhs_scale=c_scales[rows, :],
                    start=True,
                    stop=True,
                )

        part = [pool.tile([P, N], F32, name="part%d" % i) for i in range(T)]
        root = [pool.tile([P, N], F32, name="root%d" % i) for i in range(T)]
        mag = [pool.tile([P, N], F32, name="mag%d" % i) for i in range(T)]
        positive = [pool.tile([P, N], BF16, name="positive%d" % i) for i in range(T)]
        t = [pool.tile([P, N], F32, name="t%d" % i) for i in range(T)]
        y = [pool.tile([P, N], F32, name="y%d" % i) for i in range(T)]
        row_sum = [pool.tile([P, 1], F32, name="row_sum%d" % i) for i in range(T)]
        inv_sum = [pool.tile([P, 1], F32, name="inv_sum%d" % i) for i in range(T)]

        def distance(i):
            g, h = tiles[i]
            nc.vector.scalar_tensor_tensor(
                out=part[i][:], in0=z[g, h][:], scalar=bias[:, i : i + 1], in1=cn_sb[g][:], op0=ALU.add, op1=ALU.add
            )

        def inverse_root(i):
            nc.scalar.activation(out=root[i][:], in_=part[i][:], func=ACT.Abs_reciprocal_sqrt)

        def square(i):
            nc.scalar.activation(out=mag[i][:], in_=root[i][:], func=ACT.Square)

        def sign(i, engine):
            engine.tensor_scalar(
                out=positive[i][:], in0=part[i][:], scalar1=TINY, scalar2=-TINY, op0=ALU.min, op1=ALU.max
            )

        def sign_on_gpsimd(i):
            if i < SIGNS_ON_GPSIMD:
                sign(i, nc.gpsimd)

        def sign_on_vector(i):
            if i >= SIGNS_ON_GPSIMD:
                sign(i, nc.vector)

        def signed_sum(i):
            nc.vector.scalar_tensor_tensor(
                out=t[i][:], in0=positive[i][:], scalar=1.0 / TINY, in1=mag[i][:], op0=ALU.mult, op1=ALU.mult,
                accum_out=row_sum[i][:],
            )

        def invert_sum(i):
            nc.vector.reciprocal(out=inv_sum[i][:], in_=row_sum[i][:])

        def store(i):
            g, h = tiles[i]
            nc.sync.dma_start(out=out[g, h * P : (h + 1) * P, :], in_=y[i][:])

        def normalise_on_vector(i):
            if i % 2 == 1:
                nc.vector.tensor_scalar(out=y[i][:], in0=t[i][:], scalar1=inv_sum[i][:], scalar2=None, op0=ALU.mult)
                store(i)

        def normalise_on_scalar(i):
            if i % 2 == 0:
                nc.scalar.activation(out=y[i][:], in_=t[i][:], func=ACT.Copy, scale=inv_sum[i][:])
                store(i)

        stages = [
            (distance, 0),
            (sign_on_gpsimd, 0),
            (signed_sum, 6),
            (sign_on_vector, 2),
            (normalise_on_vector, 7),
            (invert_sum, 6),
            (inverse_root, 2),
            (square, 3),
            (normalise_on_scalar, 6),
        ]
        for step in range(T + 7):
            for stage, lag in stages:
                if 0 <= step - lag < T:
                    stage(step - lag)
